import numpy as np
import ml_dtypes


def mxq(x, axis, fmt="e4m3"):
    dtype, down = {"e4m3": (ml_dtypes.float8_e4m3fn, 7), "e5m2": (ml_dtypes.float8_e5m2, 14)}[fmt]
    v = np.moveaxis(np.asarray(x, np.float32).astype(ml_dtypes.bfloat16).astype(np.float64), axis, -1)
    blocks = v.reshape(v.shape[:-1] + (-1, 32))
    amax = np.abs(blocks).max(-1, keepdims=True)
    byte = np.maximum(np.where(amax > 0, np.frexp(amax)[1] - 1 + 127, 0) - down, 1)
    scale = np.exp2(byte - 127.0)
    codes = (blocks / scale).astype(np.float32).astype(dtype).astype(np.float64)
    return np.moveaxis((codes * scale).reshape(v.shape), -1, axis)


WIDE = False


def mx_kscale(k):
    if not WIDE:
        return np.ones(k)
    levels = np.array([10, -10, 5, -5, 0])
    if k % 512:
        return np.exp2(np.random.permutation(np.resize(levels, k // 32))).repeat(32)
    a = np.empty((k // 512, 16))
    for p in range(k // 512):
        a[p, :8] = np.random.permutation(np.resize(levels, 8))
        for g in range(8):
            far = levels[np.abs(levels - a[p, g]) >= 10]
            a[p, g + 8] = far[np.random.randint(len(far))]
    return np.exp2(a.ravel()).repeat(32)


def f64(x):
    return np.asarray(x).astype(np.float64)


def striped(idx):
    return np.tile(idx.reshape(-1, 16).T, (8, 1)).astype(np.uint16)


def unstriped(offs):
    return offs[:16].T.reshape(-1).astype(np.int64)


def striped8(idx):
    return np.concatenate([x.reshape(-1, 16).T for x in idx]).astype(np.uint16)


def runs(offs, k):
    lists = np.stack([offs[16 * r : 16 * r + 16].T.reshape(-1) for r in range(8)]).astype(np.int64)
    return lists[np.arange(k) % 512 // 64]


def pack_weight(w):
    k, n = w.shape
    w = f64(np.asarray(w, np.float32).astype(ml_dtypes.bfloat16)).reshape(k // 32, 32, n)
    amax = np.abs(w).max(1)
    byte = np.clip(np.where(amax > 0, np.frexp(amax)[1] - 1 + 127 - 7, 1), 1, 254)
    scaled = (w * np.exp2(127.0 - byte)[:, None, :]).reshape(k, n).astype(np.float32)
    words = np.ascontiguousarray(scaled.reshape(k // 512, 128, 4, n).transpose(0, 1, 3, 2)).astype(ml_dtypes.float8_e4m3fn).view(np.uint8)
    return words, np.ascontiguousarray(byte.astype(np.uint8).reshape(k // 512, 16, n))


def unpack_weight(words, scales):
    g, p, n, _ = words.shape
    vals = np.ascontiguousarray(words).view(ml_dtypes.float8_e4m3fn).astype(np.float64) * np.repeat(np.exp2(scales.astype(np.float64) - 127.0), 8, axis=1)[..., None]
    return vals.transpose(0, 1, 3, 2).reshape(g * 512, n)


def sigmoid(v):
    return 1.0 / (1.0 + np.exp(-np.maximum(v, -700.0)))

def planes(y):
    n, m = y.shape
    v = y.astype(np.float32).astype(ml_dtypes.bfloat16).astype(np.float64).reshape(n // 32, 32, m)
    top = np.abs(v).max(1)
    byte = np.clip(np.where(top > 0, np.frexp(top)[1] - 1 + 127 - 7, 1), 1, 254)
    codes = (v * np.exp2(127.0 - byte)[:, None, :]).reshape(n, m).astype(np.float32).astype(ml_dtypes.float8_e4m3fn).view(np.uint8)
    words = codes.reshape(n // 512, 128, 4, m).transpose(0, 1, 3, 2)
    return np.ascontiguousarray(words), np.ascontiguousarray(byte.astype(np.uint8).reshape(n // 512, 16, m))


K, T, S, H, W, C, G = 512, 1024, 512, 512, 384, 512, 2048


def setup_inputs():
    n = np.random.standard_normal
    s = mx_kscale(K)[:, None]
    packed_xT = pack_weight(n((K, T)) * s)
    packed_w1 = pack_weight(n((K, H)) / np.sqrt(K) / s)
    packed_dT = pack_weight(n((K, G)) / s)
    return {
        "x_words": packed_xT[0],
        "x_scales": packed_xT[1],
        "w1_words": packed_w1[0],
        "w1_scales": packed_w1[1],
        "gs": (np.random.uniform(0.5, 1.5, (K, 1)) / s).astype(np.float32),
        "gk": (np.random.uniform(0.5, 1.5, (K, 1)) * s).astype(np.float32),
        "d_words": packed_dT[0],
        "d_scales": packed_dT[1],
        "offs": striped(np.random.permutation(T)[:S]),
        "n1": striped(np.random.permutation(S)[:W]),
        "n2": striped(np.random.permutation(S)[:W]),
        "n3": striped(np.random.permutation(S)),
        "n4": striped(np.random.permutation(S)),
        "cand": striped(np.random.permutation(T)[:C]),
        "k1": striped8(np.random.randint(0, G, (8, H))),
        "n5": striped8(np.stack([np.random.permutation(S) for _ in range(8)])),
        "n6": striped8(np.stack([np.random.permutation(S) for _ in range(8)])),
    }


def reference(x_words, x_scales, w1_words, w1_scales, gs, gk, d_words, d_scales, offs, n1, n2, n3, n4, cand, k1, n5, n6):
    x_cand = unpack_weight(x_words, x_scales)[:, unstriped(cand)]
    xq = unpack_weight(x_words, x_scales)[:, unstriped(offs)]
    y = unpack_weight(w1_words, w1_scales).T @ xq
    pa = y[:, unstriped(n2)]
    old = y[:, unstriped(n1)]
    ra = np.minimum(pa, old) - (0.5 * pa)
    ds = y.copy()
    ds[:, unstriped(n1)] = ra
    z = f64(gs) * ds
    a = 0.0625 * ((x_cand.T @ mxq(z, 0, "e4m3")))
    d_k1 = unpack_weight(d_words, d_scales)[np.arange(K)[:, None], runs(k1, K)]
    z2 = f64(gk) * (y[:, unstriped(n3)] - y[:, unstriped(n4)])
    b = 0.0625 * ((d_k1.T @ mxq(z2, 0, "e4m3")))
    out_0 = (a + a[np.arange(C)[:, None], runs(n5, C)]) * (sigmoid(b + b[np.arange(H)[:, None], runs(n6, H)]))
    return (out_0,) + planes(out_0)

@@ -1,0 +1,263 @@
+from contextlib import ExitStack
+
+import concourse.mybir as mybir
+from concourse.masks import make_identity
+
+F32 = mybir.dt.float32
+BF16 = mybir.dt.bfloat16
+I32 = mybir.dt.int32
+U32 = mybir.dt.uint32
+U16 = mybir.dt.uint16
+U8 = mybir.dt.uint8
+FP8X4 = mybir.dt.float8_e4m3fn_x4
+ALU = mybir.AluOpType
+ACT = mybir.ActivationFunctionType
+
+P = 128
+PACK = 4
+K, T, S, H, W, C, G = 512, 1024, 512, 512, 384, 512, 2048
+HALF = S // 2
+FLOPS = 3 * 2 * 512 * 512 * 512
+
+
+def tile_picked_cdkeytriebkmingap_none_po_kernel(tc, x_words, x_scales, w1_words, w1_scales, gs, gk, d_words, d_scales,
+        offs, n1, n2, n3, n4, cand, k1, n5, n6, out_0, out_1, out_2):
+    nc = tc.nc
+    with ExitStack() as ctx:
+        held = ctx.enter_context(tc.tile_pool(name="held", bufs=1))
+        sb = ctx.enter_context(tc.tile_pool(name="sb", bufs=1))
+        psum = ctx.enter_context(tc.psum_pool(name="psum", bufs=1))
+
+        def tile(name, shape, dtype):
+            return sb.tile(shape, dtype, name=name, align_bytes=64)
+
+        def list_tile(name, src):
+            return held.tile(list(src.shape), U16, name=name)
+
+        def words_view(dram):
+            return dram[0].rearrange("p n t -> p (n t)").bitcast(I32)
+
+        def dealt(ap):
+            return ap.rearrange("p (t m) -> p m t", t=PACK)
+
+        def in_fours(ap):
+            return ap.rearrange("p (m t) -> p m t", t=PACK)
+
+        def halves(lst, h):
+            cols = lst.shape[1] // 2
+            return lst[:, h * cols:(h + 1) * cols]
+
+        lists = {}
+        for name, src in (("offs", offs), ("n1", n1), ("n2", n2), ("n3", n3), ("n4", n4), ("cand", cand), ("k1", k1), ("n5", n5), ("n6", n6)):
+            lists[name] = (list_tile("l_" + name, src), src)
+
+        def load_list(name):
+            nc.sync.dma_start(lists[name][0][:], lists[name][1])
+            return lists[name][0]
+
+        xw = tile("xw", [P, T], U32)
+        xs = tile("xs", [P, T], U8)
+        w1w = tile("w1w", [P, H], U32)
+        w1s = tile("w1s", [P, H], U8)
+        dw = tile("dw", [P, G], U32)
+        dsc = tile("dsc", [P, G], U8)
+        kse = tile("kse", [P, H], U8)
+        gs_t = tile("gs_t", [P, PACK], F32)
+        gk_t = tile("gk_t", [P, PACK], F32)
+        ident = tile("ident", [P, P], F32)
+
+        nc.vector.memset(xs[:].bitcast(I32), 0)
+        nc.vector.memset(w1s[:].bitcast(I32), 0)
+        nc.vector.memset(dsc[:].bitcast(I32), 0)
+        nc.vector.memset(kse[:].bitcast(I32), 0)
+
+        nc.sync.dma_start(xw[:].bitcast(I32), words_view(x_words))
+        l_offs = load_list("offs")
+        for r in range(4):
+            nc.sync.dma_start(xs[r:P:32, :].bitcast(I32), x_scales[0][r:16:4, :].bitcast(I32))
+        nc.sync.dma_start(w1w[:].bitcast(I32), words_view(w1_words))
+        for r in range(4):
+            nc.sync.dma_start(w1s[r:P:32, :].bitcast(I32), w1_scales[0][r:16:4, :].bitcast(I32))
+        l_cand = load_list("cand")
+        l_n3 = load_list("n3")
+        l_n4 = load_list("n4")
+        nc.sync.dma_start(dw[:].bitcast(I32), words_view(d_words))
+        l_k1 = load_list("k1")
+        for e in range(2):
+            nc.sync.dma_start(dsc[e:P:16, :].bitcast(I32), d_scales[0][e:16:2, :].bitcast(I32))
+        l_n2 = load_list("n2")
+        l_n1 = load_list("n1")
+        nc.sync.dma_start(gk_t[:], gk.rearrange("(p t) o -> p (t o)", t=PACK))
+        nc.sync.dma_start(gs_t[:], gs.rearrange("(p t) o -> p (t o)", t=PACK))
+        l_n6 = load_list("n6")
+        l_n5 = load_list("n5")
+        make_identity(nc, ident[:])
+
+        xqw = tile("xqw", [P, S], U32)
+        xqs = tile("xqs", [P, S], U8)
+        w1wd = tile("w1wd", [P, H], U32)
+        w1sd = tile("w1sd", [P, H], U8)
+        nc.vector.tensor_copy(xqw[:], xw[:].indirect(l_offs[:]))
+        nc.scalar.copy(dealt(w1wd[:]), in_fours(w1w[:]))
+        nc.vector.tensor_copy(xqs[:], xs[:].indirect(l_offs[:]))
+        nc.vector.tensor_copy(dealt(w1sd[:]), in_fours(w1s[:]))
+
+        def product(t, lw, ls, rw, rs):
+            acc = psum.tile([P, S], F32, name="acc", tag="acc", bufs=4)
+            cols = slice(t * P, (t + 1) * P)
+            nc.tensor.matmul_mx(out=acc[:], lhsT=lw[:, cols].bitcast(FP8X4), lhsT_scale=ls[:, cols],
+                                rhs=rw[:].bitcast(FP8X4), rhs_scale=rs[:], start=True, stop=True)
+            return acc
+
+        y_acc = [product(t, w1wd, w1sd, xqw, xqs) for t in range(PACK)]
+
+        cw = tile("cw", [P, C], U32)
+        cs = tile("cs", [P, C], U8)
+        kwg = tile("kwg", [P, H], U32)
+        ksg = tile("ksg", [P, H], U8)
+        kw = tile("kw", [P, H], U32)
+        ksd = tile("ksd", [P, H], U8)
+        nc.vector.tensor_copy(dealt(cw[:]), xw[:].indirect(l_cand[:]))
+        nc.vector.tensor_copy(dealt(cs[:]), xs[:].indirect(l_cand[:]))
+        nc.vector.tensor_copy(ksg[:], dsc[:].indirect(l_k1[:]))
+        nc.vector.tensor_copy(kwg[:], dw[:].indirect(l_k1[:]))
+        nc.vector.tensor_copy(dealt(ksd[:]), in_fours(ksg[:]))
+        nc.vector.tensor_copy(dealt(kw[:]), in_fours(kwg[:]))
+        for r in range(4):
+            src = 16 * (r // 2) + r % 2
+            nc.sync.dma_start(kse[r:P:32, :].bitcast(I32), ksd[src:P:32, :].bitcast(I32))
+
+        y = [tile("y%d" % t, [P, 2 * S], F32) for t in range(PACK)]
+        b = [tile("b%d" % t, [P, 2 * S], F32) for t in range(PACK)]
+        g3 = [b[t][:, S:] for t in range(PACK)]
+        g4 = tile("g4", [P, PACK, S], F32)
+        diff = tile("diff", [P, PACK, S], F32)
+        nh = [tile("nh%d" % t, [P, W], F32) for t in range(PACK)]
+        old = [tile("old%d" % t, [P, W], F32) for t in range(PACK)]
+        low = [tile("low%d" % t, [P, W], F32) for t in range(PACK)]
+        zp = tile("zp", [P, PACK, S], BF16)
+
+        def fetch34(t):
+            nc.scalar.activation(g3[t], y[t][:].indirect(l_n3[:]), ACT.Copy)
+            nc.scalar.activation(g4[:, t, :], y[t][:].indirect(l_n4[:]), ACT.Copy)
+
+        def fetch2(t):
+            nc.scalar.activation(nh[t][:], y[t][:].indirect(l_n2[:]), ACT.Copy, scale=-0.5)
+
+        def fetch1(t, on_vector):
+            if on_vector:
+                nc.vector.tensor_copy(old[t][:], y[t][:].indirect(l_n1[:]))
+            else:
+                nc.scalar.activation(old[t][:], y[t][:].indirect(l_n1[:]), ACT.Copy)
+
+        def sub(t):
+            nc.vector.tensor_tensor(diff[:, t, :], g3[t], g4[:, t, :], ALU.subtract)
+
+        def smaller(t):
+            nc.vector.scalar_tensor_tensor(low[t][:], nh[t][:], -2.0, old[t][:], ALU.mult, ALU.min)
+
+        def put(t):
+            nc.vector.tensor_tensor(y[t][:].indirect(l_n1[:]), low[t][:], nh[t][:], ALU.add)
+
+        def plane(t):
+            nc.vector.tensor_scalar(zp[:, t, :], y[t][:, :S], gs_t[:, t:t + 1], None, ALU.mult)
+
+        def woven(ap):
+            return ap.rearrange("p (c i) t -> p c t i", i=4)
+
+        def by_planes(ap):
+            return ap.rearrange("p t (c i) -> p c t i", i=4)
+
+        def quantise(words, scales, src):
+            nc.vector.quantize_mx(out=words.bitcast(FP8X4), scales=scales, in_=src.rearrange("p j t -> p (j t)"))
+
+        for t in range(PACK):
+            nc.scalar.copy(y[t][:, :S], y_acc[t][:])
+            fetch34(t)
+            if t == 0:
+                fetch2(t)
+        fetch1(0, True)
+        sub(0)
+        smaller(0)
+        sub(1)
+        put(0)
+        sub(2)
+        plane(0)
+        sub(3)
+        z2b = tile("z2b", [P, S, PACK], BF16)
+        z2w = tile("z2w", [P, S], U32)
+        z2s = tile("z2s", [P, S], U8)
+        gk_b = gk_t[:].unsqueeze(1).unsqueeze(3).broadcast_to([P, S // 4, PACK, 4])
+        nc.vector.tensor_tensor(woven(z2b[:]), by_planes(diff[:]), gk_b, ALU.mult)
+        quantise(z2w[:], z2s[:], z2b[:])
+        b_acc = [product(t, kw, kse, z2w, z2s) for t in range(PACK)]
+        for t in range(1, PACK):
+            fetch2(t)
+            fetch1(t, False)
+
+        zb = tile("zb", [P, S, PACK], BF16)
+        zw = tile("zw", [P, S], U32)
+        zs = tile("zs", [P, S], U8)
+        gb_tiles = [tile("gb%d" % t, [P, S], F32) for t in range(PACK - 1)]
+        gb = [g[:] for g in gb_tiles]
+        gb.append(zb[:].rearrange("p j t -> p (j t)")[:, :2 * S].bitcast(F32))
+        sigt = [tile("sigt%d" % t, [P, S], F32) for t in range(PACK)]
+
+        def fetch6(t):
+            nc.scalar.activation(gb[t], b[t][:].indirect(l_n6[:]), ACT.Copy)
+
+        def gate(t):
+            turned = psum.tile([P, S], F32, name="turned", tag="turned", bufs=2)
+            for jb in range(S // P):
+                cols = slice(jb * P, (jb + 1) * P)
+                nc.tensor.matmul(turned[:, cols], lhsT=b[t][:, cols], rhs=ident[:], is_transpose=True, start=True, stop=False)
+                nc.tensor.matmul(turned[:, cols], lhsT=gb[t][:, cols], rhs=ident[:], is_transpose=True, start=False, stop=True)
+            nc.scalar.activation(sigt[t][:], turned[:], ACT.Sigmoid, scale=0.0625)
+
+        for t in range(1, PACK):
+            smaller(t)
+            put(t)
+            plane(t)
+        for t in range(PACK):
+            nc.scalar.copy(b[t][:, :S], b_acc[t][:])
+            if t < PACK - 1:
+                fetch6(t)
+            if t > 0:
+                gate(t - 1)
+        nc.vector.tensor_copy(woven(zb[:]), by_planes(zp[:]))
+        quantise(zw[:], zs[:], zb[:])
+        a_acc = [product(t, cw, cs, zw, zs) for t in range(PACK)]
+        nc.vector.tensor_copy(gb[3], b[3][:].indirect(l_n6[:]))
+
+        a = [tile("a%d" % t, [P, S], F32) for t in range(PACK)]
+        ga = tile("ga", [P, PACK, S], F32)
+        tot = tile("tot", [P, PACK, S], F32)
+        res = tile("res", [P, PACK, S], F32)
+        ob = tile("ob", [P, S, PACK], BF16)
+        ow = tile("ow", [P, S], U32)
+        osc = tile("osc", [P, S], U8)
+        out_rows = out_0.rearrange("(p t) j -> p t j", t=PACK)
+        for h in range(2):
+            cols = slice(h * HALF, (h + 1) * HALF)
+            for t in range(PACK):
+                if h == 0:
+                    if t == 1:
+                        nc.vector.tensor_scalar(a[t][:], a_acc[t][:], 0.0625, None, ALU.mult)
+                    else:
+                        nc.scalar.activation(a[t][:], a_acc[t][:], ACT.Copy, scale=0.0625)
+                nc.scalar.activation(ga[:, t, cols], a[t][:].indirect(halves(l_n5, h)), ACT.Copy)
+                if h == 0 and t == 1:
+                    gate(3)
+                nc.vector.tensor_tensor(tot[:, t, cols], a[t][:, cols], ga[:, t, cols], ALU.add)
+                if t % 2 == 1:
+                    sig = psum.tile([P, 2, HALF], F32, name="sig", tag="sig", bufs=2)
+                    for u in range(2):
+                        for jb in range(2):
+                            nc.tensor.transpose(sig[:, u, jb * P:(jb + 1) * P], sigt[t - 1 + u][:, h * HALF + jb * P:h * HALF + (jb + 1) * P], ident[:])
+                    nc.vector.tensor_tensor(res[:, t - 1:t + 1, cols], tot[:, t - 1:t + 1, cols], sig[:], ALU.mult)
+                    nc.sync.dma_start(out_rows[:, t - 1:t + 1, cols], res[:, t - 1:t + 1, cols])
+            nc.vector.tensor_copy(woven(ob[:, cols, :]), by_planes(res[:, :, cols]))
+            quantise(ow[:, cols], osc[:, cols], ob[:, cols, :])
+            nc.sync.dma_start(words_view(out_1)[:, cols], ow[:, cols].bitcast(I32))
+        for r in range(4):
+            nc.sync.dma_start(out_2[0][r:16:4, :].bitcast(I32), osc[r:P:32, :].bitcast(I32))

@@ -17,6 +17,13 @@ P = 128
 PACK = 4
 K, T, S, H, W, C, G = 512, 1024, 512, 512, 384, 512, 2048
 HALF = S // 2
+LAST = PACK - 1
+PUT_S = 1
+EV_V = (0, 1, 2)
+N5_V = ()
+ADD_V = ((0, 2), (0, 3), (1, 2), (1, 3))
+PLANE_S = ()
+IL_S = (0,)
 FLOPS = 3 * 2 * 512 * 512 * 512
 
 
@@ -28,8 +35,8 @@ def tile_picked_cdkeytriebkmingap_none_po_kernel(tc, x_words, x_scales, w1_words
         sb = ctx.enter_context(tc.tile_pool(name="sb", bufs=1))
         psum = ctx.enter_context(tc.psum_pool(name="psum", bufs=1))
 
-        def tile(name, shape, dtype):
-            return sb.tile(shape, dtype, name=name, align_bytes=64)
+        def tile(name, shape, dtype, tag=None):
+            return sb.tile(shape, dtype, name=name, tag=tag or name, align_bytes=64)
 
         def list_tile(name, src):
             return held.tile(list(src.shape), U16, name=name)
@@ -66,25 +73,25 @@ def tile_picked_cdkeytriebkmingap_none_po_kernel(tc, x_words, x_scales, w1_words
         gk_t = tile("gk_t", [P, PACK], F32)
         ident = tile("ident", [P, P], F32)
 
-        nc.vector.memset(xs[:].bitcast(I32), 0)
-        nc.vector.memset(w1s[:].bitcast(I32), 0)
+        nc.gpsimd.memset(xs[:].bitcast(I32), 0)
+        nc.gpsimd.memset(w1s[:].bitcast(I32), 0)
         nc.vector.memset(dsc[:].bitcast(I32), 0)
         nc.vector.memset(kse[:].bitcast(I32), 0)
 
-        nc.sync.dma_start(xw[:].bitcast(I32), words_view(x_words))
         l_offs = load_list("offs")
         for r in range(4):
             nc.sync.dma_start(xs[r:P:32, :].bitcast(I32), x_scales[0][r:16:4, :].bitcast(I32))
+        nc.sync.dma_start(xw[:].bitcast(I32), words_view(x_words))
         nc.sync.dma_start(w1w[:].bitcast(I32), words_view(w1_words))
         for r in range(4):
             nc.sync.dma_start(w1s[r:P:32, :].bitcast(I32), w1_scales[0][r:16:4, :].bitcast(I32))
         l_cand = load_list("cand")
         l_n3 = load_list("n3")
-        l_n4 = load_list("n4")
-        nc.sync.dma_start(dw[:].bitcast(I32), words_view(d_words))
         l_k1 = load_list("k1")
         for e in range(2):
             nc.sync.dma_start(dsc[e:P:16, :].bitcast(I32), d_scales[0][e:16:2, :].bitcast(I32))
+        l_n4 = load_list("n4")
+        nc.sync.dma_start(dw[:].bitcast(I32), words_view(d_words))
         l_n2 = load_list("n2")
         l_n1 = load_list("n1")
         nc.sync.dma_start(gk_t[:], gk.rearrange("(p t) o -> p (t o)", t=PACK))
@@ -97,13 +104,13 @@ def tile_picked_cdkeytriebkmingap_none_po_kernel(tc, x_words, x_scales, w1_words
         xqs = tile("xqs", [P, S], U8)
         w1wd = tile("w1wd", [P, H], U32)
         w1sd = tile("w1sd", [P, H], U8)
+        nc.vector.tensor_copy(xqs[:], xs[:].indirect(l_offs[:]))
         nc.vector.tensor_copy(xqw[:], xw[:].indirect(l_offs[:]))
         nc.scalar.copy(dealt(w1wd[:]), in_fours(w1w[:]))
-        nc.vector.tensor_copy(xqs[:], xs[:].indirect(l_offs[:]))
         nc.vector.tensor_copy(dealt(w1sd[:]), in_fours(w1s[:]))
 
-        def product(t, lw, ls, rw, rs):
-            acc = psum.tile([P, S], F32, name="acc", tag="acc", bufs=4)
+        def product(t, lw, ls, rw, rs, tag="acc"):
+            acc = psum.tile([P, S], F32, name="acc", tag=tag, bufs=4)
             cols = slice(t * P, (t + 1) * P)
             nc.tensor.matmul_mx(out=acc[:], lhsT=lw[:, cols].bitcast(FP8X4), lhsT_scale=ls[:, cols],
                                 rhs=rw[:].bitcast(FP8X4), rhs_scale=rs[:], start=True, stop=True)
@@ -134,33 +141,40 @@ def tile_picked_cdkeytriebkmingap_none_po_kernel(tc, x_words, x_scales, w1_words
         diff = tile("diff", [P, PACK, S], F32)
         nh = [tile("nh%d" % t, [P, W], F32) for t in range(PACK)]
         old = [tile("old%d" % t, [P, W], F32) for t in range(PACK)]
-        low = [tile("low%d" % t, [P, W], F32) for t in range(PACK)]
+        low0 = tile("low0", [P, W], F32)
+        low = [low0[:]] + [diff[:, t, :W] for t in range(1, PACK)]
         zp = tile("zp", [P, PACK, S], BF16)
 
-        def fetch34(t):
-            nc.scalar.activation(g3[t], y[t][:].indirect(l_n3[:]), ACT.Copy)
-            nc.scalar.activation(g4[:, t, :], y[t][:].indirect(l_n4[:]), ACT.Copy)
+        def fetch(on_vector, out, window, offsets):
+            if on_vector:
+                nc.vector.tensor_copy(out, window.indirect(offsets))
+            else:
+                nc.scalar.activation(out, window.indirect(offsets), ACT.Copy)
 
         def fetch2(t):
             nc.scalar.activation(nh[t][:], y[t][:].indirect(l_n2[:]), ACT.Copy, scale=-0.5)
 
-        def fetch1(t, on_vector):
-            if on_vector:
-                nc.vector.tensor_copy(old[t][:], y[t][:].indirect(l_n1[:]))
-            else:
-                nc.scalar.activation(old[t][:], y[t][:].indirect(l_n1[:]), ACT.Copy)
-
         def sub(t):
-            nc.vector.tensor_tensor(diff[:, t, :], g3[t], g4[:, t, :], ALU.subtract)
+            eng = nc.vector if t >= 2 else nc.gpsimd
+            eng.tensor_tensor(diff[:, t, :], g3[t], g4[:, t, :], ALU.subtract)
 
         def smaller(t):
-            nc.vector.scalar_tensor_tensor(low[t][:], nh[t][:], -2.0, old[t][:], ALU.mult, ALU.min)
+            nc.vector.scalar_tensor_tensor(low[t], nh[t][:], -2.0, old[t][:], ALU.mult, ALU.min)
 
         def put(t):
-            nc.vector.tensor_tensor(y[t][:].indirect(l_n1[:]), low[t][:], nh[t][:], ALU.add)
+            if t == PUT_S:
+                nc.vector.tensor_tensor(old[t][:], low[t], nh[t][:], ALU.add)
+                nc.scalar.activation(y[t][:].indirect(l_n1[:]), old[t][:], ACT.Copy)
+            else:
+                nc.vector.tensor_tensor(y[t][:].indirect(l_n1[:]), low[t], nh[t][:], ALU.add)
 
         def plane(t):
-            nc.vector.tensor_scalar(zp[:, t, :], y[t][:, :S], gs_t[:, t:t + 1], None, ALU.mult)
+            if t in PLANE_S:
+                nc.scalar.activation(zp[:, t, :], y[t][:, :S], ACT.Copy, scale=gs_t[:, t:t + 1])
+            elif t >= 2:
+                nc.vector.tensor_scalar(zp[:, t, :], y[t][:, :S], gs_t[:, t:t + 1], None, ALU.mult)
+            else:
+                nc.gpsimd.tensor_scalar(zp[:, t, :], y[t][:, :S], gs_t[:, t:t + 1], 0.0, ALU.mult, ALU.add)
 
         def woven(ap):
             return ap.rearrange("p (c i) t -> p c t i", i=4)
@@ -173,17 +187,15 @@ def tile_picked_cdkeytriebkmingap_none_po_kernel(tc, x_words, x_scales, w1_words
 
         for t in range(PACK):
             nc.scalar.copy(y[t][:, :S], y_acc[t][:])
-            fetch34(t)
+        for t in (0, 3, 1, 2):
+            fetch(t == LAST, g3[t], y[t][:], l_n3[:])
+            fetch(t == LAST, g4[:, t, :], y[t][:], l_n4[:])
             if t == 0:
                 fetch2(t)
-        fetch1(0, True)
-        sub(0)
-        smaller(0)
-        sub(1)
-        put(0)
-        sub(2)
-        plane(0)
-        sub(3)
+                fetch(True, old[t][:], y[t][:], l_n1[:])
+                smaller(t)
+                put(t)
+            sub(t)
         z2b = tile("z2b", [P, S, PACK], BF16)
         z2w = tile("z2w", [P, S], U32)
         z2s = tile("z2s", [P, S], U8)
@@ -193,14 +205,14 @@ def tile_picked_cdkeytriebkmingap_none_po_kernel(tc, x_words, x_scales, w1_words
         b_acc = [product(t, kw, kse, z2w, z2s) for t in range(PACK)]
         for t in range(1, PACK):
             fetch2(t)
-            fetch1(t, False)
+            fetch(False, old[t][:], y[t][:], l_n1[:])
 
         zb = tile("zb", [P, S, PACK], BF16)
-        zw = tile("zw", [P, S], U32)
         zs = tile("zs", [P, S], U8)
-        gb_tiles = [tile("gb%d" % t, [P, S], F32) for t in range(PACK - 1)]
-        gb = [g[:] for g in gb_tiles]
-        gb.append(zb[:].rearrange("p j t -> p (j t)")[:, :2 * S].bitcast(F32))
+        gb_tiles = [tile("gb%d" % t, [P, S], F32) for t in range(2)]
+        zb_words = zb[:].rearrange("p j t -> p (j t)").bitcast(F32)
+        gb = [g[:] for g in gb_tiles] + [zb_words[:, :S], zb_words[:, S:]]
+        a = [tile("a%d" % t, [P, 2 * S], F32) for t in range(PACK)]
         sigt = [tile("sigt%d" % t, [P, S], F32) for t in range(PACK)]
 
         def fetch6(t):
@@ -212,51 +224,70 @@ def tile_picked_cdkeytriebkmingap_none_po_kernel(tc, x_words, x_scales, w1_words
                 cols = slice(jb * P, (jb + 1) * P)
                 nc.tensor.matmul(turned[:, cols], lhsT=b[t][:, cols], rhs=ident[:], is_transpose=True, start=True, stop=False)
                 nc.tensor.matmul(turned[:, cols], lhsT=gb[t][:, cols], rhs=ident[:], is_transpose=True, start=False, stop=True)
-            nc.scalar.activation(sigt[t][:], turned[:], ACT.Sigmoid, scale=0.0625)
+            nc.scalar.activation(sigt[t][:], turned[:], ACT.Tanh, scale=0.03125)
 
+        plane(0)
         for t in range(1, PACK):
             smaller(t)
             put(t)
             plane(t)
         for t in range(PACK):
             nc.scalar.copy(b[t][:, :S], b_acc[t][:])
-            if t < PACK - 1:
+            if t < 2:
                 fetch6(t)
-            if t > 0:
-                gate(t - 1)
+                gate(t)
         nc.vector.tensor_copy(woven(zb[:]), by_planes(zp[:]))
+        zw = tile("zw", [P, S], U32, tag="gb1")
         quantise(zw[:], zs[:], zb[:])
         a_acc = [product(t, cw, cs, zw, zs) for t in range(PACK)]
-        nc.vector.tensor_copy(gb[3], b[3][:].indirect(l_n6[:]))
+        for t in range(2, PACK):
+            fetch6(t)
+            gate(t)
 
-        a = [tile("a%d" % t, [P, S], F32) for t in range(PACK)]
-        ga = tile("ga", [P, PACK, S], F32)
-        tot = tile("tot", [P, PACK, S], F32)
+        ga01 = tile("ga", [P, 2, S], F32)
+        ga = [ga01[:, 0, :], ga01[:, 1, :], gb[2], gb[3]]
+        tot = tile("tot", [P, 2, S], F32)
+        tot2 = tile("tot2", [P, 2, HALF], F32)
         res = tile("res", [P, PACK, S], F32)
         ob = tile("ob", [P, S, PACK], BF16)
         ow = tile("ow", [P, S], U32)
         osc = tile("osc", [P, S], U8)
         out_rows = out_0.rearrange("(p t) j -> p t j", t=PACK)
+
+        def evict_a(t):
+            if t in EV_V:
+                nc.vector.tensor_scalar(a[t][:, :S], a_acc[t][:], 0.03125, None, ALU.mult)
+            else:
+                nc.scalar.activation(a[t][:, :S], a_acc[t][:], ACT.Copy, scale=0.03125)
+
+        def finish(ts, cols, sums):
+            width = cols.stop - cols.start
+            th = psum.tile([P, len(ts), width], F32, name="th", tag="th", bufs=2)
+            for u, t in enumerate(ts):
+                for jb in range(width // P):
+                    nc.tensor.transpose(th[:, u, jb * P:(jb + 1) * P], sigt[t][:, cols.start + jb * P:cols.start + (jb + 1) * P], ident[:])
+            rows = slice(ts[0], ts[-1] + 1)
+            nc.vector.scalar_tensor_tensor(res[:, rows, cols], th[:], 1.0, sums, ALU.add, ALU.mult)
+            nc.sync.dma_start(out_rows[:, rows, cols], res[:, rows, cols])
+
+        for t in range(PACK):
+            evict_a(t)
+        for t in range(2):
+            fetch(True, ga[t], a[t][:], l_n5[:])
+            nc.gpsimd.tensor_tensor(tot[:, t, :], a[t][:, :S], ga[t], ALU.add)
+            finish([t], slice(0, S), tot[:, t:t + 1, :])
         for h in range(2):
             cols = slice(h * HALF, (h + 1) * HALF)
-            for t in range(PACK):
-                if h == 0:
-                    if t == 1:
-                        nc.vector.tensor_scalar(a[t][:], a_acc[t][:], 0.0625, None, ALU.mult)
-                    else:
-                        nc.scalar.activation(a[t][:], a_acc[t][:], ACT.Copy, scale=0.0625)
-                nc.scalar.activation(ga[:, t, cols], a[t][:].indirect(halves(l_n5, h)), ACT.Copy)
-                if h == 0 and t == 1:
-                    gate(3)
-                nc.vector.tensor_tensor(tot[:, t, cols], a[t][:, cols], ga[:, t, cols], ALU.add)
-                if t % 2 == 1:
-                    sig = psum.tile([P, 2, HALF], F32, name="sig", tag="sig", bufs=2)
-                    for u in range(2):
-                        for jb in range(2):
-                            nc.tensor.transpose(sig[:, u, jb * P:(jb + 1) * P], sigt[t - 1 + u][:, h * HALF + jb * P:h * HALF + (jb + 1) * P], ident[:])
-                    nc.vector.tensor_tensor(res[:, t - 1:t + 1, cols], tot[:, t - 1:t + 1, cols], sig[:], ALU.mult)
-                    nc.sync.dma_start(out_rows[:, t - 1:t + 1, cols], res[:, t - 1:t + 1, cols])
-            nc.vector.tensor_copy(woven(ob[:, cols, :]), by_planes(res[:, :, cols]))
+            for t in range(2, PACK):
+                got = ga[t][:, (1 - h) * HALF:(2 - h) * HALF]
+                fetch((h, t) in N5_V, got, a[t][:], halves(l_n5, h))
+                adder = nc.vector if (h, t) in ADD_V else nc.gpsimd
+                adder.tensor_tensor(tot2[:, t - 2, :], a[t][:, cols], got, ALU.add)
+            finish([2, 3], cols, tot2[:])
+            if h in IL_S:
+                nc.scalar.copy(woven(ob[:, cols, :]), by_planes(res[:, :, cols]))
+            else:
+                nc.vector.tensor_copy(woven(ob[:, cols, :]), by_planes(res[:, :, cols]))
             quantise(ow[:, cols], osc[:, cols], ob[:, cols, :])
             nc.sync.dma_start(words_view(out_1)[:, cols], ow[:, cols].bitcast(I32))
         for r in range(4):

@@ -18,12 +18,18 @@ PACK = 4
 K, T, S, H, W, C, G = 512, 1024, 512, 512, 384, 512, 2048
 HALF = S // 2
 LAST = PACK - 1
-PUT_S = 1
-EV_V = (0, 1, 2)
-N5_V = ()
-ADD_V = ((0, 2), (0, 3), (1, 2), (1, 3))
+PUT_S = (0,)
+EV_V = (0, 1)
+N5_V = ((0, 0), (0, 1), (1, 0), (1, 1))
+ADD_V = ((1, 0), (1, 1))
 PLANE_S = ()
 IL_S = (0,)
+G_V = (0,)
+SUB_G = (0, 1, 2)
+F1_V = ()
+OLD_TAG = "old3"
+ADD_G = ()
+ZW_TAG = "gb2"
 FLOPS = 3 * 2 * 512 * 512 * 512
 
 
@@ -136,14 +142,12 @@ def tile_picked_cdkeytriebkmingap_none_po_kernel(tc, x_words, x_scales, w1_words
 
         y = [tile("y%d" % t, [P, 2 * S], F32) for t in range(PACK)]
         b = [tile("b%d" % t, [P, 2 * S], F32) for t in range(PACK)]
-        g3 = [b[t][:, S:] for t in range(PACK)]
-        g4 = tile("g4", [P, PACK, S], F32)
+        g3 = tile("g3", [P, PACK, S], F32)
+        g4 = [b[t][:, S:] for t in range(PACK)]
         diff = tile("diff", [P, PACK, S], F32)
         nh = [tile("nh%d" % t, [P, W], F32) for t in range(PACK)]
-        old = [tile("old%d" % t, [P, W], F32) for t in range(PACK)]
-        low0 = tile("low0", [P, W], F32)
-        low = [low0[:]] + [diff[:, t, :W] for t in range(1, PACK)]
-        zp = tile("zp", [P, PACK, S], BF16)
+        old = [tile("old%d" % t, [P, W], F32) for t in range(LAST)]
+        low = [diff[:, t, :W] for t in range(PACK)]
 
         def fetch(on_vector, out, window, offsets):
             if on_vector:
@@ -155,14 +159,17 @@ def tile_picked_cdkeytriebkmingap_none_po_kernel(tc, x_words, x_scales, w1_words
             nc.scalar.activation(nh[t][:], y[t][:].indirect(l_n2[:]), ACT.Copy, scale=-0.5)
 
         def sub(t):
-            eng = nc.vector if t >= 2 else nc.gpsimd
-            eng.tensor_tensor(diff[:, t, :], g3[t], g4[:, t, :], ALU.subtract)
+            if t in SUB_G:
+                fetch(True, g3[:, t, :], y[t][:], l_n3[:])
+                nc.gpsimd.tensor_tensor(diff[:, t, :], g3[:, t, :], g4[t], ALU.subtract)
+            else:
+                nc.vector.tensor_tensor(diff[:, t, :], y[t][:].indirect(l_n3[:]), g4[t], ALU.subtract)
 
         def smaller(t):
             nc.vector.scalar_tensor_tensor(low[t], nh[t][:], -2.0, old[t][:], ALU.mult, ALU.min)
 
         def put(t):
-            if t == PUT_S:
+            if t in PUT_S:
                 nc.vector.tensor_tensor(old[t][:], low[t], nh[t][:], ALU.add)
                 nc.scalar.activation(y[t][:].indirect(l_n1[:]), old[t][:], ACT.Copy)
             else:
@@ -171,10 +178,8 @@ def tile_picked_cdkeytriebkmingap_none_po_kernel(tc, x_words, x_scales, w1_words
         def plane(t):
             if t in PLANE_S:
                 nc.scalar.activation(zp[:, t, :], y[t][:, :S], ACT.Copy, scale=gs_t[:, t:t + 1])
-            elif t >= 2:
-                nc.vector.tensor_scalar(zp[:, t, :], y[t][:, :S], gs_t[:, t:t + 1], None, ALU.mult)
             else:
-                nc.gpsimd.tensor_scalar(zp[:, t, :], y[t][:, :S], gs_t[:, t:t + 1], 0.0, ALU.mult, ALU.add)
+                nc.vector.tensor_scalar(zp[:, t, :], y[t][:, :S], gs_t[:, t:t + 1], None, ALU.mult)
 
         def woven(ap):
             return ap.rearrange("p (c i) t -> p c t i", i=4)
@@ -187,14 +192,8 @@ def tile_picked_cdkeytriebkmingap_none_po_kernel(tc, x_words, x_scales, w1_words
 
         for t in range(PACK):
             nc.scalar.copy(y[t][:, :S], y_acc[t][:])
-        for t in (0, 3, 1, 2):
-            fetch(t == LAST, g3[t], y[t][:], l_n3[:])
-            fetch(t == LAST, g4[:, t, :], y[t][:], l_n4[:])
-            if t == 0:
-                fetch2(t)
-                fetch(True, old[t][:], y[t][:], l_n1[:])
-                smaller(t)
-                put(t)
+        for t in range(PACK):
+            fetch(False, g4[t], y[t][:], l_n4[:])
             sub(t)
         z2b = tile("z2b", [P, S, PACK], BF16)
         z2w = tile("z2w", [P, S], U32)
@@ -203,15 +202,15 @@ def tile_picked_cdkeytriebkmingap_none_po_kernel(tc, x_words, x_scales, w1_words
         nc.vector.tensor_tensor(woven(z2b[:]), by_planes(diff[:]), gk_b, ALU.mult)
         quantise(z2w[:], z2s[:], z2b[:])
         b_acc = [product(t, kw, kse, z2w, z2s) for t in range(PACK)]
-        for t in range(1, PACK):
+        old.append(tile("old3", [P, W], F32, tag=OLD_TAG))
+        for t in range(PACK):
             fetch2(t)
-            fetch(False, old[t][:], y[t][:], l_n1[:])
+            fetch(t in F1_V, old[t][:], y[t][:], l_n1[:])
 
         zb = tile("zb", [P, S, PACK], BF16)
         zs = tile("zs", [P, S], U8)
-        gb_tiles = [tile("gb%d" % t, [P, S], F32) for t in range(2)]
-        zb_words = zb[:].rearrange("p j t -> p (j t)").bitcast(F32)
-        gb = [g[:] for g in gb_tiles] + [zb_words[:, :S], zb_words[:, S:]]
+        gb_tiles = [tile("gb%d" % t, [P, S], F32) for t in range(PACK)]
+        gb = [g[:] for g in gb_tiles]
         a = [tile("a%d" % t, [P, 2 * S], F32) for t in range(PACK)]
         sigt = [tile("sigt%d" % t, [P, S], F32) for t in range(PACK)]
 
@@ -219,35 +218,33 @@ def tile_picked_cdkeytriebkmingap_none_po_kernel(tc, x_words, x_scales, w1_words
             nc.scalar.activation(gb[t], b[t][:].indirect(l_n6[:]), ACT.Copy)
 
         def gate(t):
-            turned = psum.tile([P, S], F32, name="turned", tag="turned", bufs=2)
+            turned = psum.tile([P, S], F32, name="turned", tag="turned", bufs=4)
             for jb in range(S // P):
                 cols = slice(jb * P, (jb + 1) * P)
                 nc.tensor.matmul(turned[:, cols], lhsT=b[t][:, cols], rhs=ident[:], is_transpose=True, start=True, stop=False)
                 nc.tensor.matmul(turned[:, cols], lhsT=gb[t][:, cols], rhs=ident[:], is_transpose=True, start=False, stop=True)
             nc.scalar.activation(sigt[t][:], turned[:], ACT.Tanh, scale=0.03125)
 
-        plane(0)
-        for t in range(1, PACK):
+        for t in range(PACK):
             smaller(t)
             put(t)
-            plane(t)
+            if t == 2:
+                zp = tile("zp", [P, PACK, S], BF16, tag="nh2")
+                for u in range(3):
+                    plane(u)
+        plane(LAST)
         for t in range(PACK):
             nc.scalar.copy(b[t][:, :S], b_acc[t][:])
-            if t < 2:
-                fetch6(t)
-                gate(t)
-        nc.vector.tensor_copy(woven(zb[:]), by_planes(zp[:]))
-        zw = tile("zw", [P, S], U32, tag="gb1")
-        quantise(zw[:], zs[:], zb[:])
-        a_acc = [product(t, cw, cs, zw, zs) for t in range(PACK)]
-        for t in range(2, PACK):
             fetch6(t)
             gate(t)
+        nc.vector.tensor_copy(woven(zb[:]), by_planes(zp[:]))
+        zw = tile("zw", [P, S], U32, tag=ZW_TAG)
+        quantise(zw[:], zs[:], zb[:])
+        a_acc = [product(t, cw, cs, zw, zs) for t in range(PACK)]
 
-        ga01 = tile("ga", [P, 2, S], F32)
-        ga = [ga01[:, 0, :], ga01[:, 1, :], gb[2], gb[3]]
-        tot = tile("tot", [P, 2, S], F32)
-        tot2 = tile("tot2", [P, 2, HALF], F32)
+        ga_all = tile("ga", [P, PACK, S], F32)
+        ga = [ga_all[:, t, :] for t in range(PACK)]
+        tot = tile("tot", [P, PACK, S], F32)
         res = tile("res", [P, PACK, S], F32)
         ob = tile("ob", [P, S, PACK], BF16)
         ow = tile("ow", [P, S], U32)
@@ -262,7 +259,7 @@ def tile_picked_cdkeytriebkmingap_none_po_kernel(tc, x_words, x_scales, w1_words
 
         def finish(ts, cols, sums):
             width = cols.stop - cols.start
-            th = psum.tile([P, len(ts), width], F32, name="th", tag="th", bufs=2)
+            th = psum.tile([P, len(ts), width], F32, name="th", tag="turned", bufs=4)
             for u, t in enumerate(ts):
                 for jb in range(width // P):
                     nc.tensor.transpose(th[:, u, jb * P:(jb + 1) * P], sigt[t][:, cols.start + jb * P:cols.start + (jb + 1) * P], ident[:])
@@ -272,18 +269,14 @@ def tile_picked_cdkeytriebkmingap_none_po_kernel(tc, x_words, x_scales, w1_words
 
         for t in range(PACK):
             evict_a(t)
-        for t in range(2):
-            fetch(True, ga[t], a[t][:], l_n5[:])
-            nc.gpsimd.tensor_tensor(tot[:, t, :], a[t][:, :S], ga[t], ALU.add)
-            finish([t], slice(0, S), tot[:, t:t + 1, :])
         for h in range(2):
             cols = slice(h * HALF, (h + 1) * HALF)
-            for t in range(2, PACK):
-                got = ga[t][:, (1 - h) * HALF:(2 - h) * HALF]
-                fetch((h, t) in N5_V, got, a[t][:], halves(l_n5, h))
+            for t in range(PACK):
+                fetch((h, t) in N5_V, ga[t][:, cols], a[t][:], halves(l_n5, h))
                 adder = nc.vector if (h, t) in ADD_V else nc.gpsimd
-                adder.tensor_tensor(tot2[:, t - 2, :], a[t][:, cols], got, ALU.add)
-            finish([2, 3], cols, tot2[:])
+                adder.tensor_tensor(tot[:, t, cols], a[t][:, cols], ga[t][:, cols], ALU.add)
+                if t % 2 == 1:
+                    finish([t - 1, t], cols, tot[:, t - 1:t + 1, cols])
             if h in IL_S:
                 nc.scalar.copy(woven(ob[:, cols, :]), by_planes(res[:, :, cols]))
             else:
@@ -291,4 +284,4 @@ def tile_picked_cdkeytriebkmingap_none_po_kernel(tc, x_words, x_scales, w1_words
             quantise(ow[:, cols], osc[:, cols], ob[:, cols, :])
             nc.sync.dma_start(words_view(out_1)[:, cols], ow[:, cols].bitcast(I32))
         for r in range(4):
-            nc.sync.dma_start(out_2[0][r:16:4, :].bitcast(I32), osc[r:P:32, :].bitcast(I32))
+            (nc.sync if r < 2 else nc.scalar).dma_start(out_2[0][r:16:4, :].bitcast(I32), osc[r:P:32, :].bitcast(I32))

@@ -15,26 +15,25 @@ ACT = mybir.ActivationFunctionType
 
 P = 128
 PACK = 4
-K, T, S, H, W, C, G = 512, 1024, 512, 512, 384, 512, 2048
-HALF = S // 2
 LAST = PACK - 1
-PUT_S = (0,)
-EV_V = (0, 1)
-N5_V = ((0, 0), (0, 1), (1, 0), (1, 1))
-ADD_V = ((1, 0), (1, 1))
-PLANE_S = ()
-IL_S = (0,)
-G_V = (0,)
-SUB_G = (0, 1, 2)
-F1_V = ()
-OLD_TAG = "old3"
-ADD_G = ()
-ZW_TAG = "gb2"
+QUADRANT = 32
+GROUP = 16
+SCALE_ROWS = 16
+T, S, H, W, C, G = 1024, 512, 512, 384, 512, 2048
 FLOPS = 3 * 2 * 512 * 512 * 512
 
+HALF_SIXTEENTH = 0.03125
+PIECE = 256
+SPLIT = 384
+SCALAR_SCATTER = 0
+SCALAR_N3 = LAST
+VECTOR_A = 2
 
-def tile_picked_cdkeytriebkmingap_none_po_kernel(tc, x_words, x_scales, w1_words, w1_scales, gs, gk, d_words, d_scales,
-        offs, n1, n2, n3, n4, cand, k1, n5, n6, out_0, out_1, out_2):
+
+def tile_picked_cdkeytriebkmingap_none_po_kernel(
+    tc, x_words, x_scales, w1_words, w1_scales, gs, gk, d_words, d_scales,
+    offs, n1, n2, n3, n4, cand, k1, n5, n6, out_0, out_1, out_2,
+):
     nc = tc.nc
     with ExitStack() as ctx:
         held = ctx.enter_context(tc.tile_pool(name="held", bufs=1))
@@ -44,11 +43,21 @@ def tile_picked_cdkeytriebkmingap_none_po_kernel(tc, x_words, x_scales, w1_words
         def tile(name, shape, dtype, tag=None):
             return sb.tile(shape, dtype, name=name, tag=tag or name, align_bytes=64)
 
-        def list_tile(name, src):
-            return held.tile(list(src.shape), U16, name=name)
+        def bank(name, shape, tag):
+            return psum.tile(shape, F32, name=name, tag=tag, bufs=PACK)
+
+        def load_list(name, src):
+            offsets = held.tile(list(src.shape), U16, name=name)
+            nc.sync.dma_start(offsets[:], src)
+            return offsets
 
         def words_view(dram):
             return dram[0].rearrange("p n t -> p (n t)").bitcast(I32)
+
+        def load_scales(dst, dram, rows_together):
+            step = P * rows_together // SCALE_ROWS
+            for r in range(rows_together):
+                nc.sync.dma_start(dst[r:P:step, :].bitcast(I32), dram[0][r:SCALE_ROWS:rows_together, :].bitcast(I32))
 
         def dealt(ap):
             return ap.rearrange("p (t m) -> p m t", t=PACK)
@@ -56,98 +65,11 @@ def tile_picked_cdkeytriebkmingap_none_po_kernel(tc, x_words, x_scales, w1_words
         def in_fours(ap):
             return ap.rearrange("p (m t) -> p m t", t=PACK)
 
-        def halves(lst, h):
-            cols = lst.shape[1] // 2
-            return lst[:, h * cols:(h + 1) * cols]
+        def woven(ap):
+            return ap.rearrange("p (c i) t -> p c t i", i=4)
 
-        lists = {}
-        for name, src in (("offs", offs), ("n1", n1), ("n2", n2), ("n3", n3), ("n4", n4), ("cand", cand), ("k1", k1), ("n5", n5), ("n6", n6)):
-            lists[name] = (list_tile("l_" + name, src), src)
-
-        def load_list(name):
-            nc.sync.dma_start(lists[name][0][:], lists[name][1])
-            return lists[name][0]
-
-        xw = tile("xw", [P, T], U32)
-        xs = tile("xs", [P, T], U8)
-        w1w = tile("w1w", [P, H], U32)
-        w1s = tile("w1s", [P, H], U8)
-        dw = tile("dw", [P, G], U32)
-        dsc = tile("dsc", [P, G], U8)
-        kse = tile("kse", [P, H], U8)
-        gs_t = tile("gs_t", [P, PACK], F32)
-        gk_t = tile("gk_t", [P, PACK], F32)
-        ident = tile("ident", [P, P], F32)
-
-        nc.gpsimd.memset(xs[:].bitcast(I32), 0)
-        nc.gpsimd.memset(w1s[:].bitcast(I32), 0)
-        nc.vector.memset(dsc[:].bitcast(I32), 0)
-        nc.vector.memset(kse[:].bitcast(I32), 0)
-
-        l_offs = load_list("offs")
-        for r in range(4):
-            nc.sync.dma_start(xs[r:P:32, :].bitcast(I32), x_scales[0][r:16:4, :].bitcast(I32))
-        nc.sync.dma_start(xw[:].bitcast(I32), words_view(x_words))
-        nc.sync.dma_start(w1w[:].bitcast(I32), words_view(w1_words))
-        for r in range(4):
-            nc.sync.dma_start(w1s[r:P:32, :].bitcast(I32), w1_scales[0][r:16:4, :].bitcast(I32))
-        l_cand = load_list("cand")
-        l_n3 = load_list("n3")
-        l_k1 = load_list("k1")
-        for e in range(2):
-            nc.sync.dma_start(dsc[e:P:16, :].bitcast(I32), d_scales[0][e:16:2, :].bitcast(I32))
-        l_n4 = load_list("n4")
-        nc.sync.dma_start(dw[:].bitcast(I32), words_view(d_words))
-        l_n2 = load_list("n2")
-        l_n1 = load_list("n1")
-        nc.sync.dma_start(gk_t[:], gk.rearrange("(p t) o -> p (t o)", t=PACK))
-        nc.sync.dma_start(gs_t[:], gs.rearrange("(p t) o -> p (t o)", t=PACK))
-        l_n6 = load_list("n6")
-        l_n5 = load_list("n5")
-        make_identity(nc, ident[:])
-
-        xqw = tile("xqw", [P, S], U32)
-        xqs = tile("xqs", [P, S], U8)
-        w1wd = tile("w1wd", [P, H], U32)
-        w1sd = tile("w1sd", [P, H], U8)
-        nc.vector.tensor_copy(xqs[:], xs[:].indirect(l_offs[:]))
-        nc.vector.tensor_copy(xqw[:], xw[:].indirect(l_offs[:]))
-        nc.scalar.copy(dealt(w1wd[:]), in_fours(w1w[:]))
-        nc.vector.tensor_copy(dealt(w1sd[:]), in_fours(w1s[:]))
-
-        def product(t, lw, ls, rw, rs, tag="acc"):
-            acc = psum.tile([P, S], F32, name="acc", tag=tag, bufs=4)
-            cols = slice(t * P, (t + 1) * P)
-            nc.tensor.matmul_mx(out=acc[:], lhsT=lw[:, cols].bitcast(FP8X4), lhsT_scale=ls[:, cols],
-                                rhs=rw[:].bitcast(FP8X4), rhs_scale=rs[:], start=True, stop=True)
-            return acc
-
-        y_acc = [product(t, w1wd, w1sd, xqw, xqs) for t in range(PACK)]
-
-        cw = tile("cw", [P, C], U32)
-        cs = tile("cs", [P, C], U8)
-        kwg = tile("kwg", [P, H], U32)
-        ksg = tile("ksg", [P, H], U8)
-        kw = tile("kw", [P, H], U32)
-        ksd = tile("ksd", [P, H], U8)
-        nc.vector.tensor_copy(dealt(cw[:]), xw[:].indirect(l_cand[:]))
-        nc.vector.tensor_copy(dealt(cs[:]), xs[:].indirect(l_cand[:]))
-        nc.vector.tensor_copy(ksg[:], dsc[:].indirect(l_k1[:]))
-        nc.vector.tensor_copy(kwg[:], dw[:].indirect(l_k1[:]))
-        nc.vector.tensor_copy(dealt(ksd[:]), in_fours(ksg[:]))
-        nc.vector.tensor_copy(dealt(kw[:]), in_fours(kwg[:]))
-        for r in range(4):
-            src = 16 * (r // 2) + r % 2
-            nc.sync.dma_start(kse[r:P:32, :].bitcast(I32), ksd[src:P:32, :].bitcast(I32))
-
-        y = [tile("y%d" % t, [P, 2 * S], F32) for t in range(PACK)]
-        b = [tile("b%d" % t, [P, 2 * S], F32) for t in range(PACK)]
-        g3 = tile("g3", [P, PACK, S], F32)
-        g4 = [b[t][:, S:] for t in range(PACK)]
-        diff = tile("diff", [P, PACK, S], F32)
-        nh = [tile("nh%d" % t, [P, W], F32) for t in range(PACK)]
-        old = [tile("old%d" % t, [P, W], F32) for t in range(LAST)]
-        low = [diff[:, t, :W] for t in range(PACK)]
+        def by_planes(ap):
+            return ap.rearrange("p t (c i) -> p c t i", i=4)
 
         def fetch(on_vector, out, window, offsets):
             if on_vector:
@@ -155,133 +77,178 @@ def tile_picked_cdkeytriebkmingap_none_po_kernel(tc, x_words, x_scales, w1_words
             else:
                 nc.scalar.activation(out, window.indirect(offsets), ACT.Copy)
 
-        def fetch2(t):
-            nc.scalar.activation(nh[t][:], y[t][:].indirect(l_n2[:]), ACT.Copy, scale=-0.5)
-
-        def sub(t):
-            if t in SUB_G:
-                fetch(True, g3[:, t, :], y[t][:], l_n3[:])
-                nc.gpsimd.tensor_tensor(diff[:, t, :], g3[:, t, :], g4[t], ALU.subtract)
-            else:
-                nc.vector.tensor_tensor(diff[:, t, :], y[t][:].indirect(l_n3[:]), g4[t], ALU.subtract)
-
-        def smaller(t):
-            nc.vector.scalar_tensor_tensor(low[t], nh[t][:], -2.0, old[t][:], ALU.mult, ALU.min)
-
-        def put(t):
-            if t in PUT_S:
-                nc.vector.tensor_tensor(old[t][:], low[t], nh[t][:], ALU.add)
-                nc.scalar.activation(y[t][:].indirect(l_n1[:]), old[t][:], ACT.Copy)
-            else:
-                nc.vector.tensor_tensor(y[t][:].indirect(l_n1[:]), low[t], nh[t][:], ALU.add)
-
-        def plane(t):
-            if t in PLANE_S:
-                nc.scalar.activation(zp[:, t, :], y[t][:, :S], ACT.Copy, scale=gs_t[:, t:t + 1])
-            else:
-                nc.vector.tensor_scalar(zp[:, t, :], y[t][:, :S], gs_t[:, t:t + 1], None, ALU.mult)
-
-        def woven(ap):
-            return ap.rearrange("p (c i) t -> p c t i", i=4)
-
-        def by_planes(ap):
-            return ap.rearrange("p t (c i) -> p c t i", i=4)
-
         def quantise(words, scales, src):
             nc.vector.quantize_mx(out=words.bitcast(FP8X4), scales=scales, in_=src.rearrange("p j t -> p (j t)"))
 
+        def product(lhs_words, lhs_scales, rhs_words, rhs_scales):
+            planes = []
+            for t in range(PACK):
+                acc = bank("acc", [P, S], "acc")
+                cols = slice(t * P, (t + 1) * P)
+                nc.tensor.matmul_mx(
+                    out=acc[:], lhsT=lhs_words[:, cols].bitcast(FP8X4), lhsT_scale=lhs_scales[:, cols],
+                    rhs=rhs_words[:].bitcast(FP8X4), rhs_scale=rhs_scales[:], start=True, stop=True,
+                )
+                planes.append(acc)
+            return planes
+
+        x_w = tile("x_w", [P, T], U32)
+        x_s = tile("x_s", [P, T], U8)
+        w1_w = tile("w1_w", [P, H], U32)
+        w1_s = tile("w1_s", [P, H], U8)
+        d_w = tile("d_w", [P, G], U32)
+        d_s = tile("d_s", [P, G], U8)
+        key_s = tile("key_s", [P, H], U8)
+        gs_t = tile("gs_t", [P, PACK], F32)
+        gk_t = tile("gk_t", [P, PACK], F32)
+        ident = tile("ident", [P, P], F32)
+
+        nc.gpsimd.memset(x_s[:].bitcast(I32), 0)
+        nc.gpsimd.memset(w1_s[:].bitcast(I32), 0)
+        nc.vector.memset(d_s[:].bitcast(I32), 0)
+        nc.vector.memset(key_s[:].bitcast(I32), 0)
+
+        l_offs = load_list("l_offs", offs)
+        load_scales(x_s, x_scales, 4)
+        nc.sync.dma_start(x_w[:].bitcast(I32), words_view(x_words))
+        nc.sync.dma_start(w1_w[:].bitcast(I32), words_view(w1_words))
+        load_scales(w1_s, w1_scales, 4)
+        l_cand = load_list("l_cand", cand)
+        nc.sync.dma_start(d_w[:].bitcast(I32), words_view(d_words))
+        l_k1 = load_list("l_k1", k1)
+        load_scales(d_s, d_scales, 2)
+        l_n4 = load_list("l_n4", n4)
+        l_n3 = load_list("l_n3", n3)
+        l_n2 = load_list("l_n2", n2)
+        l_n1 = load_list("l_n1", n1)
+        nc.sync.dma_start(gk_t[:], gk.rearrange("(p t) o -> p (t o)", t=PACK))
+        nc.sync.dma_start(gs_t[:], gs.rearrange("(p t) o -> p (t o)", t=PACK))
+        l_n6 = load_list("l_n6", n6)
+        l_n5 = load_list("l_n5", n5)
+        make_identity(nc, ident[:])
+
+        xq_w = tile("xq_w", [P, S], U32)
+        xq_s = tile("xq_s", [P, S], U8)
+        w1_wd = tile("w1_wd", [P, H], U32)
+        w1_sd = tile("w1_sd", [P, H], U8)
+        nc.vector.tensor_copy(xq_s[:], x_s[:].indirect(l_offs[:]))
+        nc.vector.tensor_copy(xq_w[:], x_w[:].indirect(l_offs[:]))
+        nc.scalar.copy(dealt(w1_wd[:]), in_fours(w1_w[:]))
+        nc.vector.tensor_copy(dealt(w1_sd[:]), in_fours(w1_s[:]))
+        y_acc = product(w1_wd, w1_sd, xq_w, xq_s)
+
+        cand_w = tile("cand_w", [P, C], U32)
+        cand_s = tile("cand_s", [P, C], U8)
+        key_wg = tile("key_wg", [P, H], U32)
+        key_sg = tile("key_sg", [P, H], U8)
+        key_w = tile("key_w", [P, H], U32)
+        key_sd = tile("key_sd", [P, H], U8)
+        nc.vector.tensor_copy(dealt(cand_w[:]), x_w[:].indirect(l_cand[:]))
+        nc.vector.tensor_copy(dealt(cand_s[:]), x_s[:].indirect(l_cand[:]))
+        nc.vector.tensor_copy(key_sg[:], d_s[:].indirect(l_k1[:]))
+        nc.vector.tensor_copy(key_wg[:], d_w[:].indirect(l_k1[:]))
+        nc.vector.tensor_copy(dealt(key_sd[:]), in_fours(key_sg[:]))
+        nc.vector.tensor_copy(dealt(key_w[:]), in_fours(key_wg[:]))
+        for r in range(4):
+            src = GROUP * (r // 2) + r % 2
+            nc.sync.dma_start(key_s[r:P:QUADRANT, :].bitcast(I32), key_sd[src:P:QUADRANT, :].bitcast(I32))
+
+        y = [tile("y%d" % t, [P, 2 * S], F32) for t in range(PACK)]
+        b = [tile("b%d" % t, [P, 2 * S], F32) for t in range(PACK)]
+        y_n4 = [b[t][:, S:] for t in range(PACK)]
+        y_n3 = tile("y_n3", [P, S], F32)
+        diff = tile("diff", [P, PACK, S], F32)
         for t in range(PACK):
             nc.scalar.copy(y[t][:, :S], y_acc[t][:])
         for t in range(PACK):
-            fetch(False, g4[t], y[t][:], l_n4[:])
-            sub(t)
-        z2b = tile("z2b", [P, S, PACK], BF16)
-        z2w = tile("z2w", [P, S], U32)
-        z2s = tile("z2s", [P, S], U8)
-        gk_b = gk_t[:].unsqueeze(1).unsqueeze(3).broadcast_to([P, S // 4, PACK, 4])
-        nc.vector.tensor_tensor(woven(z2b[:]), by_planes(diff[:]), gk_b, ALU.mult)
-        quantise(z2w[:], z2s[:], z2b[:])
-        b_acc = [product(t, kw, kse, z2w, z2s) for t in range(PACK)]
-        old.append(tile("old3", [P, W], F32, tag=OLD_TAG))
+            fetch(False, y_n4[t], y[t][:], l_n4[:])
+            if t == SCALAR_N3:
+                fetch(False, y_n3[:], y[t][:], l_n3[:])
+                nc.vector.tensor_tensor(diff[:, t, :], y_n3[:], y_n4[t], ALU.subtract)
+            else:
+                nc.vector.tensor_tensor(diff[:, t, :], y[t][:].indirect(l_n3[:]), y_n4[t], ALU.subtract)
+        z2_b = tile("z2_b", [P, S, PACK], BF16)
+        z2_w = tile("z2_w", [P, S], U32)
+        z2_s = tile("z2_s", [P, S], U8)
+        gk_wide = gk_t[:].unsqueeze(1).unsqueeze(3).broadcast_to([P, S // 4, PACK, 4])
+        nc.vector.tensor_tensor(woven(z2_b[:]), by_planes(diff[:]), gk_wide, ALU.mult)
+        quantise(z2_w[:], z2_s[:], z2_b[:])
+        b_acc = product(key_w, key_s, z2_w, z2_s)
+
+        neg_half = [tile("neg_half%d" % t, [P, W], F32) for t in range(PACK)]
+        old = [tile("old%d" % t, [P, W], F32) for t in range(PACK)]
+        low = [diff[:, t, :W] for t in range(PACK)]
         for t in range(PACK):
-            fetch2(t)
-            fetch(t in F1_V, old[t][:], y[t][:], l_n1[:])
-
-        zb = tile("zb", [P, S, PACK], BF16)
-        zs = tile("zs", [P, S], U8)
-        gb_tiles = [tile("gb%d" % t, [P, S], F32) for t in range(PACK)]
-        gb = [g[:] for g in gb_tiles]
-        a = [tile("a%d" % t, [P, 2 * S], F32) for t in range(PACK)]
-        sigt = [tile("sigt%d" % t, [P, S], F32) for t in range(PACK)]
-
-        def fetch6(t):
-            nc.scalar.activation(gb[t], b[t][:].indirect(l_n6[:]), ACT.Copy)
-
-        def gate(t):
-            turned = psum.tile([P, S], F32, name="turned", tag="turned", bufs=4)
-            for jb in range(S // P):
-                cols = slice(jb * P, (jb + 1) * P)
-                nc.tensor.matmul(turned[:, cols], lhsT=b[t][:, cols], rhs=ident[:], is_transpose=True, start=True, stop=False)
-                nc.tensor.matmul(turned[:, cols], lhsT=gb[t][:, cols], rhs=ident[:], is_transpose=True, start=False, stop=True)
-            nc.scalar.activation(sigt[t][:], turned[:], ACT.Tanh, scale=0.03125)
-
+            nc.scalar.activation(neg_half[t][:], y[t][:].indirect(l_n2[:]), ACT.Copy, scale=-0.5)
+            fetch(False, old[t][:], y[t][:], l_n1[:])
         for t in range(PACK):
-            smaller(t)
-            put(t)
-            if t == 2:
-                zp = tile("zp", [P, PACK, S], BF16, tag="nh2")
-                for u in range(3):
-                    plane(u)
-        plane(LAST)
+            nc.vector.scalar_tensor_tensor(low[t], neg_half[t][:], -2.0, old[t][:], ALU.mult, ALU.min)
+            if t == SCALAR_SCATTER:
+                nc.vector.tensor_tensor(old[t][:], low[t], neg_half[t][:], ALU.add)
+                nc.scalar.activation(y[t][:].indirect(l_n1[:]), old[t][:], ACT.Copy)
+            else:
+                nc.vector.tensor_tensor(y[t][:].indirect(l_n1[:]), low[t], neg_half[t][:], ALU.add)
+            if t == LAST - 1:
+                z_planes = tile("z_planes", [P, PACK, S], BF16, tag="neg_half%d" % t)
+                for u in range(LAST):
+                    nc.vector.tensor_scalar(z_planes[:, u, :], y[u][:, :S], gs_t[:, u:u + 1], None, ALU.mult)
+        nc.vector.tensor_scalar(z_planes[:, LAST, :], y[LAST][:, :S], gs_t[:, LAST:], None, ALU.mult)
+
+        b_n6 = [tile("b_n6_%d" % t, [P, S], F32) for t in range(PACK)]
+        gate_t = [tile("gate_t%d" % t, [P, S], F32) for t in range(PACK)]
         for t in range(PACK):
             nc.scalar.copy(b[t][:, :S], b_acc[t][:])
-            fetch6(t)
-            gate(t)
-        nc.vector.tensor_copy(woven(zb[:]), by_planes(zp[:]))
-        zw = tile("zw", [P, S], U32, tag=ZW_TAG)
-        quantise(zw[:], zs[:], zb[:])
-        a_acc = [product(t, cw, cs, zw, zs) for t in range(PACK)]
-
-        ga_all = tile("ga", [P, PACK, S], F32)
-        ga = [ga_all[:, t, :] for t in range(PACK)]
-        tot = tile("tot", [P, PACK, S], F32)
-        res = tile("res", [P, PACK, S], F32)
-        ob = tile("ob", [P, S, PACK], BF16)
-        ow = tile("ow", [P, S], U32)
-        osc = tile("osc", [P, S], U8)
-        out_rows = out_0.rearrange("(p t) j -> p t j", t=PACK)
-
-        def evict_a(t):
-            if t in EV_V:
-                nc.vector.tensor_scalar(a[t][:, :S], a_acc[t][:], 0.03125, None, ALU.mult)
-            else:
-                nc.scalar.activation(a[t][:, :S], a_acc[t][:], ACT.Copy, scale=0.03125)
-
-        def finish(ts, cols, sums):
-            width = cols.stop - cols.start
-            th = psum.tile([P, len(ts), width], F32, name="th", tag="turned", bufs=4)
-            for u, t in enumerate(ts):
-                for jb in range(width // P):
-                    nc.tensor.transpose(th[:, u, jb * P:(jb + 1) * P], sigt[t][:, cols.start + jb * P:cols.start + (jb + 1) * P], ident[:])
-            rows = slice(ts[0], ts[-1] + 1)
-            nc.vector.scalar_tensor_tensor(res[:, rows, cols], th[:], 1.0, sums, ALU.add, ALU.mult)
-            nc.sync.dma_start(out_rows[:, rows, cols], res[:, rows, cols])
-
+            fetch(False, b_n6[t][:], b[t][:], l_n6[:])
         for t in range(PACK):
-            evict_a(t)
-        for h in range(2):
-            cols = slice(h * HALF, (h + 1) * HALF)
-            for t in range(PACK):
-                fetch((h, t) in N5_V, ga[t][:, cols], a[t][:], halves(l_n5, h))
-                adder = nc.vector if (h, t) in ADD_V else nc.gpsimd
-                adder.tensor_tensor(tot[:, t, cols], a[t][:, cols], ga[t][:, cols], ALU.add)
-                if t % 2 == 1:
-                    finish([t - 1, t], cols, tot[:, t - 1:t + 1, cols])
-            if h in IL_S:
-                nc.scalar.copy(woven(ob[:, cols, :]), by_planes(res[:, :, cols]))
+            turned = bank("turned", [P, S], "turned")
+            for j0 in range(0, S, P):
+                cols = slice(j0, j0 + P)
+                nc.tensor.matmul(turned[:, cols], lhsT=b[t][:, cols], rhs=ident[:], is_transpose=True, start=True, stop=False)
+                nc.tensor.matmul(turned[:, cols], lhsT=b_n6[t][:, cols], rhs=ident[:], is_transpose=True, start=False, stop=True)
+            nc.scalar.activation(gate_t[t][:], turned[:], ACT.Tanh, scale=HALF_SIXTEENTH)
+
+        z_b = tile("z_b", [P, S, PACK], BF16)
+        z_s = tile("z_s", [P, S], U8)
+        nc.vector.tensor_copy(woven(z_b[:]), by_planes(z_planes[:]))
+        z_w = tile("z_w", [P, S], U32, tag="b_n6_%d" % (LAST - 1))
+        quantise(z_w[:], z_s[:], z_b[:])
+        a_acc = product(cand_w, cand_s, z_w, z_s)
+        a = [tile("a%d" % t, [P, S], F32) for t in range(PACK)]
+        for t in range(PACK):
+            if t < VECTOR_A:
+                nc.vector.tensor_scalar(a[t][:], a_acc[t][:], HALF_SIXTEENTH, None, ALU.mult)
             else:
-                nc.vector.tensor_copy(woven(ob[:, cols, :]), by_planes(res[:, :, cols]))
-            quantise(ow[:, cols], osc[:, cols], ob[:, cols, :])
-            nc.sync.dma_start(words_view(out_1)[:, cols], ow[:, cols].bitcast(I32))
+                nc.scalar.activation(a[t][:], a_acc[t][:], ACT.Copy, scale=HALF_SIXTEENTH)
+
+        a_n5 = tile("a_n5", [P, PACK, S], F32)
+        total = tile("total", [P, PACK, S], F32)
+        res = tile("res", [P, PACK, S], F32)
+        out_b = tile("out_b", [P, S, PACK], BF16)
+        out_w = tile("out_w", [P, S], U32)
+        out_s = tile("out_s", [P, S], U8)
+        out_rows = out_0.rearrange("(p t) j -> p t j", t=PACK)
+        for lo, hi in ((0, SPLIT), (SPLIT, S)):
+            cols = slice(lo, hi)
+            together = S // (hi - lo)
+            for t in range(PACK):
+                for c0 in range(lo, hi, PIECE):
+                    c1 = min(c0 + PIECE, hi)
+                    fetch(c0 == 0 and t < VECTOR_A, a_n5[:, t, c0:c1], a[t][:], l_n5[:, c0 // GROUP:c1 // GROUP])
+                nc.vector.tensor_tensor(total[:, t, cols], a[t][:, cols], a_n5[:, t, cols], ALU.add)
+                if (t + 1) % together == 0:
+                    rows = slice(t + 1 - together, t + 1)
+                    gate = bank("gate", [P, together, hi - lo], "turned")
+                    for u in range(together):
+                        for j0 in range(lo, hi, P):
+                            nc.tensor.transpose(gate[:, u, j0 - lo:j0 - lo + P], gate_t[rows.start + u][:, j0:j0 + P], ident[:])
+                    nc.vector.scalar_tensor_tensor(res[:, rows, cols], gate[:], 1.0, total[:, rows, cols], ALU.add, ALU.mult)
+                    nc.sync.dma_start(out_rows[:, rows, cols], res[:, rows, cols])
+            if lo == 0:
+                nc.scalar.copy(woven(out_b[:, cols, :]), by_planes(res[:, :, cols]))
+            else:
+                nc.vector.tensor_copy(woven(out_b[:, cols, :]), by_planes(res[:, :, cols]))
+            quantise(out_w[:, cols], out_s[:, cols], out_b[:, cols, :])
+            nc.sync.dma_start(words_view(out_1)[:, cols], out_w[:, cols].bitcast(I32))
         for r in range(4):
-            (nc.sync if r < 2 else nc.scalar).dma_start(out_2[0][r:16:4, :].bitcast(I32), osc[r:P:32, :].bitcast(I32))
+            queue = nc.sync if r < 2 else nc.scalar
+            queue.dma_start(out_2[0][r:SCALE_ROWS:4, :].bitcast(I32), out_s[r:P:QUADRANT, :].bitcast(I32))

from contextlib import ExitStack

import concourse.mybir as mybir
from concourse.masks import make_identity

F32 = mybir.dt.float32
BF16 = mybir.dt.bfloat16
I32 = mybir.dt.int32
U32 = mybir.dt.uint32
U16 = mybir.dt.uint16
U8 = mybir.dt.uint8
FP8X4 = mybir.dt.float8_e4m3fn_x4
ALU = mybir.AluOpType
ACT = mybir.ActivationFunctionType

P = 128
PACK = 4
LAST = PACK - 1
QUADRANT = 32
GROUP = 16
SCALE_ROWS = 16
T, S, H, W, C, G = 1024, 512, 512, 384, 512, 2048
FLOPS = 3 * 2 * 512 * 512 * 512

HALF_SIXTEENTH = 0.03125
PIECE = 256
SPLIT = 384
SCALAR_SCATTER = 0
SCALAR_N3 = LAST
VECTOR_A = 2


def tile_picked_cdkeytriebkmingap_none_po_kernel(
    tc, x_words, x_scales, w1_words, w1_scales, gs, gk, d_words, d_scales,
    offs, n1, n2, n3, n4, cand, k1, n5, n6, out_0, out_1, out_2,
):
    nc = tc.nc
    with ExitStack() as ctx:
        held = ctx.enter_context(tc.tile_pool(name="held", bufs=1))
        sb = ctx.enter_context(tc.tile_pool(name="sb", bufs=1))
        psum = ctx.enter_context(tc.psum_pool(name="psum", bufs=1))

        def tile(name, shape, dtype, tag=None):
            return sb.tile(shape, dtype, name=name, tag=tag or name, align_bytes=64)

        def bank(name, shape, tag):
            return psum.tile(shape, F32, name=name, tag=tag, bufs=PACK)

        def load_list(name, src):
            offsets = held.tile(list(src.shape), U16, name=name)
            nc.sync.dma_start(offsets[:], src)
            return offsets

        def words_view(dram):
            return dram[0].rearrange("p n t -> p (n t)").bitcast(I32)

        def load_scales(dst, dram, rows_together):
            step = P * rows_together // SCALE_ROWS
            for r in range(rows_together):
                nc.sync.dma_start(dst[r:P:step, :].bitcast(I32), dram[0][r:SCALE_ROWS:rows_together, :].bitcast(I32))

        def dealt(ap):
            return ap.rearrange("p (t m) -> p m t", t=PACK)

        def in_fours(ap):
            return ap.rearrange("p (m t) -> p m t", t=PACK)

        def woven(ap):
            return ap.rearrange("p (c i) t -> p c t i", i=4)

        def by_planes(ap):
            return ap.rearrange("p t (c i) -> p c t i", i=4)

        def fetch(on_vector, out, window, offsets):
            if on_vector:
                nc.vector.tensor_copy(out, window.indirect(offsets))
            else:
                nc.scalar.activation(out, window.indirect(offsets), ACT.Copy)

        def quantise(words, scales, src):
            nc.vector.quantize_mx(out=words.bitcast(FP8X4), scales=scales, in_=src.rearrange("p j t -> p (j t)"))

        def product(lhs_words, lhs_scales, rhs_words, rhs_scales):
            planes = []
            for t in range(PACK):
                acc = bank("acc", [P, S], "acc")
                cols = slice(t * P, (t + 1) * P)
                nc.tensor.matmul_mx(
                    out=acc[:], lhsT=lhs_words[:, cols].bitcast(FP8X4), lhsT_scale=lhs_scales[:, cols],
                    rhs=rhs_words[:].bitcast(FP8X4), rhs_scale=rhs_scales[:], start=True, stop=True,
                )
                planes.append(acc)
            return planes

        x_w = tile("x_w", [P, T], U32)
        x_s = tile("x_s", [P, T], U8)
        w1_w = tile("w1_w", [P, H], U32)
        w1_s = tile("w1_s", [P, H], U8)
        d_w = tile("d_w", [P, G], U32)
        d_s = tile("d_s", [P, G], U8)
        key_s = tile("key_s", [P, H], U8)
        gs_t = tile("gs_t", [P, PACK], F32)
        gk_t = tile("gk_t", [P, PACK], F32)
        ident = tile("ident", [P, P], F32)

        nc.gpsimd.memset(x_s[:].bitcast(I32), 0)
        nc.gpsimd.memset(w1_s[:].bitcast(I32), 0)
        nc.vector.memset(d_s[:].bitcast(I32), 0)
        nc.vector.memset(key_s[:].bitcast(I32), 0)

        l_offs = load_list("l_offs", offs)
        load_scales(x_s, x_scales, 4)
        nc.sync.dma_start(x_w[:].bitcast(I32), words_view(x_words))
        nc.sync.dma_start(w1_w[:].bitcast(I32), words_view(w1_words))
        load_scales(w1_s, w1_scales, 4)
        l_cand = load_list("l_cand", cand)
        nc.sync.dma_start(d_w[:].bitcast(I32), words_view(d_words))
        l_k1 = load_list("l_k1", k1)
        load_scales(d_s, d_scales, 2)
        l_n4 = load_list("l_n4", n4)
        l_n3 = load_list("l_n3", n3)
        l_n2 = load_list("l_n2", n2)
        l_n1 = load_list("l_n1", n1)
        nc.sync.dma_start(gk_t[:], gk.rearrange("(p t) o -> p (t o)", t=PACK))
        nc.sync.dma_start(gs_t[:], gs.rearrange("(p t) o -> p (t o)", t=PACK))
        l_n6 = load_list("l_n6", n6)
        l_n5 = load_list("l_n5", n5)
        make_identity(nc, ident[:])

        xq_w = tile("xq_w", [P, S], U32)
        xq_s = tile("xq_s", [P, S], U8)
        w1_wd = tile("w1_wd", [P, H], U32)
        w1_sd = tile("w1_sd", [P, H], U8)
        nc.vector.tensor_copy(xq_s[:], x_s[:].indirect(l_offs[:]))
        nc.vector.tensor_copy(xq_w[:], x_w[:].indirect(l_offs[:]))
        nc.scalar.copy(dealt(w1_wd[:]), in_fours(w1_w[:]))
        nc.vector.tensor_copy(dealt(w1_sd[:]), in_fours(w1_s[:]))
        y_acc = product(w1_wd, w1_sd, xq_w, xq_s)

        cand_w = tile("cand_w", [P, C], U32)
        cand_s = tile("cand_s", [P, C], U8)
        key_wg = tile("key_wg", [P, H], U32)
        key_sg = tile("key_sg", [P, H], U8)
        key_w = tile("key_w", [P, H], U32)
        key_sd = tile("key_sd", [P, H], U8)
        nc.vector.tensor_copy(dealt(cand_w[:]), x_w[:].indirect(l_cand[:]))
        nc.vector.tensor_copy(dealt(cand_s[:]), x_s[:].indirect(l_cand[:]))
        nc.vector.tensor_copy(key_sg[:], d_s[:].indirect(l_k1[:]))
        nc.vector.tensor_copy(key_wg[:], d_w[:].indirect(l_k1[:]))
        nc.vector.tensor_copy(dealt(key_sd[:]), in_fours(key_sg[:]))
        nc.vector.tensor_copy(dealt(key_w[:]), in_fours(key_wg[:]))
        for r in range(4):
            src = GROUP * (r // 2) + r % 2
            nc.sync.dma_start(key_s[r:P:QUADRANT, :].bitcast(I32), key_sd[src:P:QUADRANT, :].bitcast(I32))

        y = [tile("y%d" % t, [P, 2 * S], F32) for t in range(PACK)]
        b = [tile("b%d" % t, [P, 2 * S], F32) for t in range(PACK)]
        y_n4 = [b[t][:, S:] for t in range(PACK)]
        y_n3 = tile("y_n3", [P, S], F32)
        diff = tile("diff", [P, PACK, S], F32)
        for t in range(PACK):
            nc.scalar.copy(y[t][:, :S], y_acc[t][:])
        for t in range(PACK):
            fetch(False, y_n4[t], y[t][:], l_n4[:])
            if t == SCALAR_N3:
                fetch(False, y_n3[:], y[t][:], l_n3[:])
                nc.vector.tensor_tensor(diff[:, t, :], y_n3[:], y_n4[t], ALU.subtract)
            else:
                nc.vector.tensor_tensor(diff[:, t, :], y[t][:].indirect(l_n3[:]), y_n4[t], ALU.subtract)
        z2_b = tile("z2_b", [P, S, PACK], BF16)
        z2_w = tile("z2_w", [P, S], U32)
        z2_s = tile("z2_s", [P, S], U8)
        gk_wide = gk_t[:].unsqueeze(1).unsqueeze(3).broadcast_to([P, S // 4, PACK, 4])
        nc.vector.tensor_tensor(woven(z2_b[:]), by_planes(diff[:]), gk_wide, ALU.mult)
        quantise(z2_w[:], z2_s[:], z2_b[:])
        b_acc = product(key_w, key_s, z2_w, z2_s)

        neg_half = [tile("neg_half%d" % t, [P, W], F32) for t in range(PACK)]
        old = [tile("old%d" % t, [P, W], F32) for t in range(PACK)]
        low = [diff[:, t, :W] for t in range(PACK)]
        for t in range(PACK):
            nc.scalar.activation(neg_half[t][:], y[t][:].indirect(l_n2[:]), ACT.Copy, scale=-0.5)
            fetch(False, old[t][:], y[t][:], l_n1[:])
        for t in range(PACK):
            nc.vector.scalar_tensor_tensor(low[t], neg_half[t][:], -2.0, old[t][:], ALU.mult, ALU.min)
            if t == SCALAR_SCATTER:
                nc.vector.tensor_tensor(old[t][:], low[t], neg_half[t][:], ALU.add)
                nc.scalar.activation(y[t][:].indirect(l_n1[:]), old[t][:], ACT.Copy)
            else:
                nc.vector.tensor_tensor(y[t][:].indirect(l_n1[:]), low[t], neg_half[t][:], ALU.add)
            if t == LAST - 1:
                z_planes = tile("z_planes", [P, PACK, S], BF16, tag="neg_half%d" % t)
                for u in range(LAST):
                    nc.vector.tensor_scalar(z_planes[:, u, :], y[u][:, :S], gs_t[:, u:u + 1], None, ALU.mult)
        nc.vector.tensor_scalar(z_planes[:, LAST, :], y[LAST][:, :S], gs_t[:, LAST:], None, ALU.mult)

        b_n6 = [tile("b_n6_%d" % t, [P, S], F32) for t in range(PACK)]
        gate_t = [tile("gate_t%d" % t, [P, S], F32) for t in range(PACK)]
        for t in range(PACK):
            nc.scalar.copy(b[t][:, :S], b_acc[t][:])
            fetch(False, b_n6[t][:], b[t][:], l_n6[:])
        for t in range(PACK):
            turned = bank("turned", [P, S], "turned")
            for j0 in range(0, S, P):
                cols = slice(j0, j0 + P)
                nc.tensor.matmul(turned[:, cols], lhsT=b[t][:, cols], rhs=ident[:], is_transpose=True, start=True, stop=False)
                nc.tensor.matmul(turned[:, cols], lhsT=b_n6[t][:, cols], rhs=ident[:], is_transpose=True, start=False, stop=True)
            nc.scalar.activation(gate_t[t][:], turned[:], ACT.Tanh, scale=HALF_SIXTEENTH)

        z_b = tile("z_b", [P, S, PACK], BF16)
        z_s = tile("z_s", [P, S], U8)
        nc.vector.tensor_copy(woven(z_b[:]), by_planes(z_planes[:]))
        z_w = tile("z_w", [P, S], U32, tag="b_n6_%d" % (LAST - 1))
        quantise(z_w[:], z_s[:], z_b[:])
        a_acc = product(cand_w, cand_s, z_w, z_s)
        a = [tile("a%d" % t, [P, S], F32) for t in range(PACK)]
        for t in range(PACK):
            if t < VECTOR_A:
                nc.vector.tensor_scalar(a[t][:], a_acc[t][:], HALF_SIXTEENTH, None, ALU.mult)
            else:
                nc.scalar.activation(a[t][:], a_acc[t][:], ACT.Copy, scale=HALF_SIXTEENTH)

        a_n5 = tile("a_n5", [P, PACK, S], F32)
        total = tile("total", [P, PACK, S], F32)
        res = tile("res", [P, PACK, S], F32)
        out_b = tile("out_b", [P, S, PACK], BF16)
        out_w = tile("out_w", [P, S], U32)
        out_s = tile("out_s", [P, S], U8)
        out_rows = out_0.rearrange("(p t) j -> p t j", t=PACK)
        for lo, hi in ((0, SPLIT), (SPLIT, S)):
            cols = slice(lo, hi)
            together = S // (hi - lo)
            for t in range(PACK):
                for c0 in range(lo, hi, PIECE):
                    c1 = min(c0 + PIECE, hi)
                    fetch(c0 == 0 and t < VECTOR_A, a_n5[:, t, c0:c1], a[t][:], l_n5[:, c0 // GROUP:c1 // GROUP])
                nc.vector.tensor_tensor(total[:, t, cols], a[t][:, cols], a_n5[:, t, cols], ALU.add)
                if (t + 1) % together == 0:
                    rows = slice(t + 1 - together, t + 1)
                    gate = bank("gate", [P, together, hi - lo], "turned")
                    for u in range(together):
                        for j0 in range(lo, hi, P):
                            nc.tensor.transpose(gate[:, u, j0 - lo:j0 - lo + P], gate_t[rows.start + u][:, j0:j0 + P], ident[:])
                    nc.vector.scalar_tensor_tensor(res[:, rows, cols], gate[:], 1.0, total[:, rows, cols], ALU.add, ALU.mult)
                    nc.sync.dma_start(out_rows[:, rows, cols], res[:, rows, cols])
            if lo == 0:
                nc.scalar.copy(woven(out_b[:, cols, :]), by_planes(res[:, :, cols]))
            else:
                nc.vector.tensor_copy(woven(out_b[:, cols, :]), by_planes(res[:, :, cols]))
            quantise(out_w[:, cols], out_s[:, cols], out_b[:, cols, :])
            nc.sync.dma_start(words_view(out_1)[:, cols], out_w[:, cols].bitcast(I32))
        for r in range(4):
            queue = nc.sync if r < 2 else nc.scalar
            queue.dma_start(out_2[0][r:SCALE_ROWS:4, :].bitcast(I32), out_s[r:P:QUADRANT, :].bitcast(I32))
